import numpy as np, ml_dtypes
CORES = [40,64,80,88,96,104,120,144]
N = 8
import mx_ref
BF = ml_dtypes.bfloat16
def entries(a):
    return np.ascontiguousarray(a.T).reshape(-1)
def table(e):
    return np.ascontiguousarray(np.reshape(e, (-1, 16)).T).astype(np.int32)
def cut(t, i, w=512):
    return t[:, w * i:w * i + w]
def f(rng, *shape):
    return mx_ref.flush((rng.standard_normal(shape, dtype=np.float32) * np.exp2(rng.integers(-2, 3, shape[:-1] + (1,)))).astype(BF))
def wide(rng, *shape, cols=0):
    v = rng.standard_normal(shape, dtype=np.float32) * np.exp2(rng.integers(-12, 13, shape)).astype(np.float32)
    if cols: v *= np.repeat(np.exp2(rng.integers(-cols, cols + 1, shape[:-2] + (1, shape[-1] // 4))) * (rng.random(shape[:-2] + (1, shape[-1] // 4)) > 0.0625), 4, axis=-1).astype(np.float32)
    return mx_ref.flush(v.astype(BF))
T, S, CAPP, O = 256, 256, 64, 2
def counts(rng, zero=0.125, quiet=()):
    send = [r for r in range(N) if r not in quiet]
    n = np.zeros((N, N), int)
    for d in range(N): n[send[rng.integers(0, len(send))], d] = 16
    for k in rng.permutation(N * N):
        r, d = k // N, k % N
        if r in send and rng.random() > zero: n[r, d] += min(rng.integers(0, CAPP + 1), CAPP - n[r, d], T - n[r].sum(), S - n[:, d].sum())
    return n
def stored(n):
    return np.stack([table(np.concatenate([n[r], np.zeros(16 - N, int)])) for r in range(N)])
def setup_inputs(rng):
    return {"x": f(rng, N, 128, 4 * T), "cn": stored(counts(rng)), "w": f(rng, N, 128, 512 * O)}
def setup_inputs_full(rng):
    n = np.zeros((N, N), int); a, b = rng.permutation(N), rng.permutation(N)
    for i in range(N):
        for j in range(min(T // CAPP, S // CAPP, N)): n[a[i], b[(i + j) % N]] = CAPP
    return {**setup_inputs(rng), "cn": stored(n)}
def setup_inputs_none(rng):
    n = counts(rng, zero=0.6, quiet=(int(rng.integers(0, N)),)); n[:, rng.integers(0, N)] = 0
    return {**setup_inputs(rng), "cn": stored(n)}
def setup_inputs_skew(rng):
    n = rng.integers(0, 4, (N, N)); n[rng.integers(0, N, N), np.arange(N)] = 4
    d = rng.integers(0, N); n[:, d] = 0; n[(d + rng.integers(1, N)) % N, d] = CAPP
    while n[:, d].sum() < S:
        q = rng.integers(0, N)
        if n[q, d] < CAPP: n[q, d] += 1
    return {**setup_inputs(rng), "cn": stored(n)}
def setup_inputs_last(rng):
    n = np.zeros((N, N), int)
    for r in (N - 2, N - 1):
        n[r] = 1
        while n[r].sum() < T:
            q = rng.integers(0, N)
            if n[r, q] < CAPP: n[r, q] += 1
    return {**setup_inputs(rng), "cn": stored(n)}
def setup_inputs_spread(rng):
    d = setup_inputs(rng); d["x"] = wide(rng, N, 128, 4 * T, cols=8); return d
def check_inputs(d):
    b = []
    e = np.stack([entries(d["cn"][r]) for r in range(N)]).astype(np.int64); n = e[:, :N]
    if n.min() < 0 or n.max() > CAPP: b.append("count")
    if (e[:, N:] != 0).any(): b.append("zeros")
    if (n.sum(axis=1) > T).any(): b.append("sent")
    if (n.sum(axis=0) > S).any(): b.append("received")
    return b
def reference(x, cn, w):
    n = np.stack([entries(cn[r])[:N] for r in range(N)])
    y = np.zeros((N, 128, O * S), np.float32); ln = np.zeros((N, 1, N + 1), np.float32)
    for d in range(N):
        ln[d, 0, 1:] = np.add.accumulate(n[:, d])
        k = int(np.add.reduce(n[:, d])); t = np.zeros((128, 4 * S), BF); at = 0
        for s in range(N):
            a, m = int(np.add.reduce(n[s, :d])), int(n[s, d])
            t[:, 4 * at:4 * (at + m)] = x[s][:, 4 * a:4 * (a + m)]; at += m
        q = mx_ref.quantize(t)
        for o in range(O): y[d][:, S * o:S * o + k] = mx_ref.matmul(mx_ref.quantize(np.ascontiguousarray(cut(w[d], o))), q)[:, :k]
    return {"y": y, "ln": ln}

@@ -1,0 +1,319 @@
+from concourse.bass import DstId, RemoteDMATransfer
+from concourse.mybir import AluOpType, ActivationFunctionType, dt
+
+CAP = 64
+NR = 8
+NX = 256
+ZC = NR * CAP
+
+SCRATCH = {
+    "xt": ("sbuf", [128, 4 * NX], "bfloat16"),
+    "wt": ("sbuf", [128, 1024], "bfloat16"),
+    "zt": ("sbuf", [128, 512], "bfloat16"),
+    "xq": ("sbuf", [128, NX + 128], "float8_e4m3fn_x4"),
+    "xs": ("sbuf", [128, NX + 128], "uint8"),
+    "wq": ("sbuf", [128, 256], "float8_e4m3fn_x4"),
+    "wsc": ("sbuf", [128, 256], "uint8"),
+    "sq": ("sbuf", [128, 7 * CAP], "float8_e4m3fn_x4"),
+    "ss": ("sbuf", [128, 7 * CAP], "uint8"),
+    "hq": ("sbuf", [128, 2 * CAP], "float8_e4m3fn_x4"),
+    "hs": ("sbuf", [128, 4 * CAP], "uint8"),
+    "hc": ("sbuf", [128, 1], "int32"),
+    "lq": ("sbuf", [128, ZC + 128], "float8_e4m3fn_x4"),
+    "ls": ("sbuf", [128, ZC + 128], "uint8"),
+    "aq": ("sbuf", [128, NX], "float8_e4m3fn_x4"),
+    "asc": ("sbuf", [128, NX], "uint8"),
+    "cnr": ("sbuf", [1, 16], "int32"),
+    "bc": ("sbuf", [128, 8], "int32"),
+    "rc": ("sbuf", [128, 32], "int32"),
+    "pidx": ("sbuf", [128, 1], "int32"),
+    "pmi": ("sbuf", [128, 1], "int32"),
+    "pmf": ("sbuf", [128, 1], "float32"),
+    "jj": ("sbuf", [128, 16], "float32"),
+    "ii": ("sbuf", [128, 16], "float32"),
+    "cf": ("sbuf", [128, 8], "float32"),
+    "pse": ("sbuf", [128, 9], "float32"),
+    "lsend": ("sbuf", [128, 32], "uint16"),
+    "rf": ("sbuf", [128, 8], "float32"),
+    "pl": ("sbuf", [128, 9], "float32"),
+    "dd": ("sbuf", [128, 8], "float32"),
+    "mk": ("sbuf", [128, 128], "float32"),
+    "t1": ("sbuf", [128, 64], "float32"),
+    "t2": ("sbuf", [128, 32], "float32"),
+    "t3": ("sbuf", [128, 16], "float32"),
+    "t4": ("sbuf", [128, 16], "float32"),
+    "lrec": ("sbuf", [128, 16], "uint16"),
+    "ysb": ("sbuf", [128, 512], "float32"),
+    "ps": ("psum", [128, 2048], "float32"),
+}
+SEMAPHORES = ["v", "cnl", "xl", "wl", "gi", "bcd", "qx", "qw", "pcx", "pdx", "psx", "psd", "own", "owns", "pref",
+              "fa", "fb", "ga", "gb", "m0a", "m1a", "m0b", "m1b", "s0", "s1", "v0", "v1", "lnd", "yd", "zd",
+              "sent", "cnt", "cod", "sca", "hci", "hqi", "hsi", "lr"]
+
+
+def bits(engines):
+    return sum(1 << e for e in engines)
+
+
+def plan(core_r, T, topo):
+    cores = T.cores
+    r = T.rank_of(core_r)
+    turn = [(r + k) % NR for k in range(1, NR)]
+    direct = [d for d in turn if topo.may_write(core_r, cores[d])]
+    cross = [d for d in range(NR) if d != r and d not in direct]
+    mine = sorted(direct + [r]).index(r)
+    cross = cross[mine:] + cross[:mine]
+    relays = [h for h in topo.cores_of(core_r) if h != core_r and all(topo.may_write(h, cores[d]) for d in cross)]
+    far = [h for h in relays if topo.die(h) != topo.die(core_r)]
+    near = [h for h in relays if topo.die(h) == topo.die(core_r)]
+    return direct, cross, far, near
+
+
+def share(engines, n):
+    k = 1
+    while 2 * k * n <= len(engines):
+        k *= 2
+    return [engines[i * k:(i + 1) * k] for i in range(n)]
+
+
+def rank_program(g, core, T, topo):
+    rank = T.rank_of(core)
+    if rank is None:
+        for c in T.cores:
+            if core in topo.cores_of(c):
+                relay_program(g, core, c, T, topo)
+        return
+    ADD, GE, MULT, MIN, MAX = AluOpType.add, AluOpType.is_ge, AluOpType.mult, AluOpType.min, AluOpType.max
+    COPY = ActivationFunctionType.Copy
+    V, A, P, Y, S = g.vector, g.scalar, g.tensor, g.sync, T.sem
+    direct, cross, far, near = plan(core, T, topo)
+    order = cross + direct + [rank]
+    w32 = dt.uint32
+
+    A.dma_start(T.xt[:], T.x[:]).then_inc(S.xl, 16)
+    Y.dma_start(T.cnr[0:1, 0:16], T.cn[:]).then_inc(S.cnl, 16)
+    Y.wait_ge(S.cnl, 16)
+    Y.dma_start(T.wt[:], T.w[:]).then_inc(S.wl, 16)
+
+    g.iota(T.pidx[:], [[1, 1]], 0, 1).then_inc(S.gi, 1)
+    g.iota(T.jj[:], [[16, 16]], 0, 0, allow_small_or_imprecise_dtypes=True).then_inc(S.gi, 1)
+    g.wait_ge(S.cnl, 16)
+    g.partition_broadcast(T.bc[:], T.cnr[0:1, 0:8], 128).then_inc(S.bcd, 1)
+    g.wait_ge(S.bcd, 1)
+    sent = [0]
+
+    def xfer(dst_core, dst, src, engines, sem):
+        rid, pid = topo.addr(dst_core, core)
+        sent[0] += len(engines)
+        return RemoteDMATransfer(dst_ids=[DstId(rid=rid, pnc=pid)], dma_engine_mask=bits(engines), remote_sem=sem,
+                                 srcs=[src], dsts=[dst])
+
+    off = topo.engines(core, T.cores[direct[0]])
+    onc = topo.engines(core, far[0])
+    tr = []
+    for k, d in enumerate(direct):
+        tr.append(xfer(T.cores[d], T.rc[:, 4 * rank:4 * rank + 1], T.bc[:, d:d + 1], off[2 * k:2 * k + 2], S.cnt))
+    rest = [e for e in onc if e not in off[:2 * len(direct)]]
+    for k, (d, h) in enumerate(zip(cross, far + near)):
+        part = rest[2 * k:2 * k + 2] if k < len(cross) - 1 else rest[2 * k:2 * k + 4]
+        tr.append(xfer(h, T.hc[:], T.bc[:, d:d + 1], part, S.hci))
+    g.remote_dma_fused(tr, local_sem=S.sent)
+
+    nv = [0]
+
+    def v(inst):
+        inst.then_inc(S.v, 1)
+        nv[0] += 1
+
+    def vw():
+        V.wait_ge(S.v, nv[0])
+
+    v(V.memset(T.zt[:], 0.0))
+    v(V.memset(T.pse[:, 0:1], 0.0))
+    v(V.memset(T.pl[:, 0:1], 0.0))
+    vw()
+    v(V.quantize_mx(T.xq[:, NX:NX + 128], T.xs[:, NX:NX + 128], T.zt[:]))
+    v(V.quantize_mx(T.lq[:, ZC:ZC + 128], T.ls[:, ZC:ZC + 128], T.zt[:]))
+    V.wait_ge(S.gi, 2)
+    v(V.tensor_scalar(T.pmi[:], T.pidx[:], 15, None, AluOpType.bitwise_and))
+    vw()
+    v(V.tensor_copy(T.pmf[:], T.pmi[:]))
+    vw()
+    v(V.tensor_scalar(T.ii[:], T.jj[:], T.pmf[:], None, ADD))
+    V.wait_ge(S.bcd, 1)
+    v(V.tensor_copy(T.cf[:], T.bc[:]))
+    v(V.tensor_copy(T.rc[:, 4 * rank:4 * rank + 1], T.bc[:, rank:rank + 1]))
+    vw()
+    v(V.tensor_tensor_scan(T.pse[:, 1:9], T.cf[:], T.cf[:], 0.0, ADD, MAX))
+    vw()
+    for k, d in enumerate(order):
+        v(V.tensor_scalar(T.lsend[:, 4 * k:4 * k + 4], T.ii[:, 0:4], T.pse[:, d:d + 1], None, ADD))
+    V.wait_ge(S.xl, 16)
+    vw()
+    V.quantize_mx(T.xq[:, 0:NX], T.xs[:, 0:NX], T.xt[:]).then_inc(S.qx, 1)
+    V.wait_ge(S.qx, 1)
+
+    nc = CAP * len(cross)
+    nd = CAP * len(direct)
+    win = NX + 128
+    cuts = [(0, nc, 0, nc // 16), (nc, nc + nd, nc // 16, (nc + nd) // 16)]
+    lo = (nc + nd) // 16
+    for (a, b, e, f), sem in zip(cuts, (S.pcx, S.pdx)):
+        V.tensor_copy(T.sq[:, a:b].bitcast(w32), T.xq[:, 0:win].bitcast(w32).indirect(T.lsend[:, e:f])).then_inc(sem, 1)
+    V.tensor_copy(T.lq[:, CAP * rank:CAP * rank + CAP].bitcast(w32),
+                  T.xq[:, 0:win].bitcast(w32).indirect(T.lsend[:, lo:lo + 4])).then_inc(S.own, 1)
+    A.wait_ge(S.qx, 1)
+    for (a, b, e, f), sem in zip(cuts, (S.psx, S.psd)):
+        A.activation(T.ss[:, a:b], T.xs[:, 0:win].indirect(T.lsend[:, e:f]), COPY).then_inc(sem, 1)
+    A.activation(T.ls[:, CAP * rank:CAP * rank + CAP], T.xs[:, 0:win].indirect(T.lsend[:, lo:lo + 4]), COPY).then_inc(S.owns, 1)
+
+    half = len(onc) // 2
+    g.wait_ge(S.pcx, 1)
+    g.remote_dma_fused([xfer(far[k], T.hq[:].bitcast(dt.uint8), T.sq[:, 2 * CAP * k:2 * CAP * (k + 1)].bitcast(dt.uint8),
+                             onc[half * k:half * (k + 1)], S.hqi) for k in range(2)], local_sem=S.sent)
+    g.wait_ge(S.psx, 1)
+    g.wait_ge(S.psd, 1)
+    g.remote_dma_fused([xfer(near[k], T.hs[:], T.ss[:, 3 * CAP * k:3 * CAP * k + 4 * CAP], onc[half * k:half * (k + 1)], S.hsi)
+                        for k in range(2)], local_sem=S.sent)
+    g.wait_ge(S.pdx, 1)
+    for k, d in enumerate(direct):
+        rid, pid = topo.addr(T.cores[d], core)
+        sent[0] += len(off)
+        g.remote_dma(T.lq[:, CAP * rank:CAP * rank + CAP].bitcast(dt.uint8),
+                     T.sq[:, nc + CAP * k:nc + CAP * k + CAP].bitcast(dt.uint8), S.cod, S.sent, pid, rid, bits(off))
+    g.wait_ge(S.sent, sent[0])
+
+    V.wait_ge(S.wl, 16)
+    V.quantize_mx(T.wq[:], T.wsc[:], T.wt[:]).then_inc(S.qw, 1)
+    ncnt, ncod, nsca = arriving(rank, T, topo)
+    V.wait_ge(S.cnt, ncnt)
+    vw()
+    v(V.tensor_copy(T.rf[:], T.rc[:, 0:32:4]))
+    vw()
+    V.tensor_tensor_scan(T.pl[:, 1:9], T.rf[:], T.rf[:], 0.0, ADD, MAX).then_inc(S.pref, 1)
+    v(V.tensor_scalar(T.dd[:], T.rf[:], -1.0, float(CAP), MULT, ADD))
+    vw()
+    V.wait_ge(S.pref, 1)
+    for s in range(NR):
+        v(V.tensor_scalar(T.mk[:, 16 * s:16 * s + 16], T.ii[:], T.pl[:, s + 1:s + 2], T.dd[:, s:s + 1], GE, MULT))
+    vw()
+    v(V.tensor_tensor(T.t1[:], T.mk[:, 0:64], T.mk[:, 64:128], ADD))
+    vw()
+    v(V.tensor_tensor(T.t2[:], T.t1[:, 0:32], T.t1[:, 32:64], ADD))
+    vw()
+    v(V.tensor_tensor(T.t3[:], T.t2[:, 0:16], T.t2[:, 16:32], ADD))
+    vw()
+    v(V.tensor_tensor(T.t4[:], T.t3[:], T.ii[:], ADD))
+    vw()
+    V.tensor_scalar(T.lrec[:], T.t4[:], float(ZC), None, MIN).then_inc(S.lr, 1)
+
+    Y.wait_ge(S.pref, 1)
+    Y.dma_start(T.ln[:], T.pl[0:1, 0:9]).then_inc(S.lnd, 16)
+
+    lw = ZC + 128
+    V.wait_ge(S.own, 1)
+    V.wait_ge(S.lr, 1)
+    V.wait_ge(S.cod, ncod)
+    for h, sem in enumerate((S.fa, S.fb)):
+        V.tensor_copy(T.aq[:, 128 * h:128 * h + 128].bitcast(w32),
+                      T.lq[:, 0:lw].bitcast(w32).indirect(T.lrec[:, 8 * h:8 * h + 8])).then_inc(sem, 1)
+    A.wait_ge(S.owns, 1)
+    A.wait_ge(S.lr, 1)
+    A.wait_ge(S.sca, nsca)
+    for h, sem in enumerate((S.ga, S.gb)):
+        A.activation(T.asc[:, 128 * h:128 * h + 128], T.ls[:, 0:lw].indirect(T.lrec[:, 8 * h:8 * h + 8]), COPY).then_inc(sem, 1)
+
+    P.wait_ge(S.qw, 1)
+    for h, (f1, g1, sems) in enumerate(((S.fa, S.ga, (S.m0a, S.m1a)), (S.fb, S.gb, (S.m0b, S.m1b)))):
+        P.wait_ge(f1, 1)
+        P.wait_ge(g1, 1)
+        for o in range(2):
+            bank = 512 * (2 * h + o)
+            P.matmul_mx(T.ps[:, bank:bank + 128], T.wq[:, 128 * o:128 * o + 128], T.wsc[:, 128 * o:128 * o + 128],
+                        T.aq[:, 128 * h:128 * h + 128], T.asc[:, 128 * h:128 * h + 128], True, True).then_inc(sems[o], 1)
+
+    for o, (m, s) in enumerate(((S.m0a, S.s0), (S.m1a, S.s1))):
+        A.wait_ge(m, 1)
+        A.activation(T.ysb[:, 256 * o:256 * o + 128], T.ps[:, 512 * o:512 * o + 128], COPY).then_inc(s, 1)
+    for o, (m, s) in enumerate(((S.m0b, S.v0), (S.m1b, S.v1))):
+        V.wait_ge(m, 1)
+        V.tensor_copy(T.ysb[:, 256 * o + 128:256 * o + 256], T.ps[:, 1024 + 512 * o:1024 + 512 * o + 128]).then_inc(s, 1)
+    Y.wait_ge(S.s0, 1)
+    Y.wait_ge(S.v0, 1)
+    Y.dma_start(T.y[:, 0:256], T.ysb[:, 0:256]).then_inc(S.yd, 16)
+    A.wait_ge(S.s1, 1)
+    A.wait_ge(S.v1, 1)
+    A.dma_start(T.y[:, 256:512], T.ysb[:, 256:512]).then_inc(S.zd, 16)
+    Y.wait_ge(S.yd, 16)
+    Y.wait_ge(S.lnd, 16)
+    A.wait_ge(S.zd, 16)
+    vw()
+
+
+def forwards(core_r, T, topo):
+    direct, cross, far, near = plan(core_r, T, topo)
+    out = {}
+    for k in range(2):
+        out[far[k]] = (cross[k], [("codes", i, cross[2 * k + i]) for i in range(2)])
+    out[near[0]] = (cross[2], [("scales", i, d) for i, d in enumerate(cross)])
+    out[near[1]] = (cross[3], [("scales", 1 + i, d) for i, d in enumerate(direct)])
+    return out
+
+
+def relay_engines(h, jobs, T, topo):
+    return share(topo.engines(h, T.cores[jobs[0][2]]), len(jobs))
+
+
+def arriving(rank, T, topo):
+    ncnt = ncod = nsca = 0
+    for s, c in enumerate(T.cores):
+        if s == rank:
+            continue
+        direct, cross, far, near = plan(c, T, topo)
+        if rank in direct:
+            ncnt += 2
+            ncod += len(topo.engines(c, T.cores[rank]))
+        for h, (cd, jobs) in forwards(c, T, topo).items():
+            if cd == rank:
+                ncnt += len(topo.engines(h, T.cores[rank]))
+            for (kind, slot, d), e in zip(jobs, relay_engines(h, jobs, T, topo)):
+                if d == rank and kind == "codes":
+                    ncod += len(e)
+                elif d == rank:
+                    nsca += len(e)
+    return ncnt, ncod, nsca
+
+
+def relay_program(g, core, home, T, topo):
+    work = forwards(home, T, topo)
+    if core not in work:
+        return
+    S = T.sem
+    src_rank = T.rank_of(home)
+    cd, jobs = work[core]
+    direct, cross, far, near = plan(home, T, topo)
+    onc = topo.engines(home, core)
+    half = len(onc) // 2
+    idx = (far + near).index(core)
+    g.wait_ge(S.hci, 2 if idx < 3 else 4)
+    dst = T.cores[cd]
+    rid, pid = topo.addr(dst, core)
+    eng = topo.engines(core, dst)
+    g.remote_dma(T.rc[:, 4 * src_rank:4 * src_rank + 1], T.hc[:], S.cnt, S.sent, pid, rid, bits(eng))
+    total = len(eng)
+    codes = jobs[0][0] == "codes"
+    g.wait_ge(S.hqi if codes else S.hsi, half)
+    tr = []
+    for (kind, slot, d), e in zip(jobs, relay_engines(core, jobs, T, topo)):
+        rid, pid = topo.addr(T.cores[d], core)
+        a, b = CAP * slot, CAP * slot + CAP
+        p, q = CAP * src_rank, CAP * src_rank + CAP
+        if codes:
+            src, dst, sem = T.hq[:, a:b].bitcast(dt.uint8), T.lq[:, p:q].bitcast(dt.uint8), S.cod
+        else:
+            src, dst, sem = T.hs[:, a:b], T.ls[:, p:q], S.sca
+        total += len(e)
+        tr.append(RemoteDMATransfer(dst_ids=[DstId(rid=rid, pnc=pid)], dma_engine_mask=bits(e), remote_sem=sem,
+                                    srcs=[src], dsts=[dst]))
+    g.remote_dma_fused(tr, local_sem=S.sent)
+    g.wait_ge(S.sent, total)

@@ -5,54 +5,38 @@ CAP = 64
 NR = 8
 NX = 256
 ZC = NR * CAP
+SG = NR + 1
 
-SCRATCH = {
-    "xt": ("sbuf", [128, 4 * NX], "bfloat16"),
-    "wt": ("sbuf", [128, 1024], "bfloat16"),
-    "zt": ("sbuf", [128, 512], "bfloat16"),
-    "xq": ("sbuf", [128, NX + 128], "float8_e4m3fn_x4"),
-    "xs": ("sbuf", [128, NX + 128], "uint8"),
-    "wq": ("sbuf", [128, 256], "float8_e4m3fn_x4"),
-    "wsc": ("sbuf", [128, 256], "uint8"),
-    "sq": ("sbuf", [128, 7 * CAP], "float8_e4m3fn_x4"),
-    "ss": ("sbuf", [128, 7 * CAP], "uint8"),
-    "hq": ("sbuf", [128, 2 * CAP], "float8_e4m3fn_x4"),
-    "hs": ("sbuf", [128, 4 * CAP], "uint8"),
-    "hc": ("sbuf", [128, 1], "int32"),
-    "lq": ("sbuf", [128, ZC + 128], "float8_e4m3fn_x4"),
-    "ls": ("sbuf", [128, ZC + 128], "uint8"),
-    "aq": ("sbuf", [128, NX], "float8_e4m3fn_x4"),
-    "asc": ("sbuf", [128, NX], "uint8"),
-    "cnr": ("sbuf", [1, 16], "int32"),
-    "bc": ("sbuf", [128, 8], "int32"),
-    "rc": ("sbuf", [128, 32], "int32"),
-    "pidx": ("sbuf", [128, 1], "int32"),
-    "pmi": ("sbuf", [128, 1], "int32"),
-    "pmf": ("sbuf", [128, 1], "float32"),
-    "jj": ("sbuf", [128, 16], "float32"),
-    "ii": ("sbuf", [128, 16], "float32"),
-    "cf": ("sbuf", [128, 8], "float32"),
-    "pse": ("sbuf", [128, 9], "float32"),
-    "lsend": ("sbuf", [128, 32], "uint16"),
-    "rf": ("sbuf", [128, 8], "float32"),
-    "pl": ("sbuf", [128, 9], "float32"),
-    "dd": ("sbuf", [128, 8], "float32"),
-    "mk": ("sbuf", [128, 128], "float32"),
-    "t1": ("sbuf", [128, 64], "float32"),
-    "t2": ("sbuf", [128, 32], "float32"),
-    "t3": ("sbuf", [128, 16], "float32"),
-    "t4": ("sbuf", [128, 16], "float32"),
-    "lrec": ("sbuf", [128, 16], "uint16"),
-    "ysb": ("sbuf", [128, 512], "float32"),
-    "ps": ("psum", [128, 2048], "float32"),
-}
-SEMAPHORES = ["v", "cnl", "xl", "wl", "gi", "bcd", "qx", "qw", "pcx", "pdx", "psx", "psd", "own", "owns", "pref",
+F8, U8, F32, I32, BF = "float8_e4m3fn_x4", "uint8", "float32", "int32", "bfloat16"
+SCRATCH = {name: ("sbuf", [p, n], d) for name, p, n, d in (
+    ("xt", 128, 4 * NX, BF), ("wt", 128, 1024, BF), ("zt", 128, 512, BF),
+    ("xq", 128, NX + 128, F8), ("xs", 128, NX + 128, U8),
+    ("wq", 128, 256, F8), ("wsc", 128, 256, U8),
+    ("sq", 128, 7 * CAP, F8), ("ss", 128, 7 * CAP, U8),
+    ("hq", 128, 2 * CAP, F8), ("hs", 128, 4 * CAP, U8), ("hc", 128, 1, I32),
+    ("lq", 128, ZC + 128, F8), ("ls", 128, ZC + 128, U8),
+    ("aq", 128, NX, F8), ("asc", 128, NX, U8),
+    ("cnr", 1, 16, I32), ("bc", 128, 8, I32), ("rc", 128, 32, I32),
+    ("pidx", 128, 1, I32), ("pmi", 128, 1, I32), ("pmf", 128, 1, F32), ("jj", 128, 16, F32), ("ii", 128, 16, F32),
+    ("cf", 128, 8, F32), ("pse", 128, 9, F32), ("lsend", 128, 28, "uint16"), ("lown", 128, 4, "uint16"),
+    ("rf", 128, 8, F32), ("pl", 128, 9, F32), ("dd", 128, 8, F32),
+    ("mk", 128, 16 * SG, F32), ("sg", 128, 16 * SG, F32), ("sc", 128, 16 * SG, F32), ("lrec", 128, 16, "uint16"),
+    ("ysb", 128, 512, F32))}
+SCRATCH["ps"] = ("psum", [128, 2048], F32)
+SEMAPHORES = ["v", "cnl", "xl", "wl", "gi", "bcd", "qx", "qw", "pcx", "pdx", "psx", "psd", "own", "owns", "pref", "ld", "lo",
               "fa", "fb", "ga", "gb", "m0a", "m1a", "m0b", "m1b", "s0", "s1", "v0", "v1", "lnd", "yd", "zd",
               "sent", "cnt", "cod", "sca", "hci", "hqi", "hsi", "lr"]
 
 
 def bits(engines):
     return sum(1 << e for e in engines)
+
+
+def share(engines, n):
+    k = 1
+    while 2 * k * n <= len(engines):
+        k *= 2
+    return [engines[i * k:(i + 1) * k] for i in range(n)]
 
 
 def plan(core_r, T, topo):
@@ -69,11 +53,46 @@ def plan(core_r, T, topo):
     return direct, cross, far, near
 
 
-def share(engines, n):
-    k = 1
-    while 2 * k * n <= len(engines):
-        k *= 2
-    return [engines[i * k:(i + 1) * k] for i in range(n)]
+def forwards(core_r, T, topo):
+    direct, cross, far, near = plan(core_r, T, topo)
+    out = {}
+    for k in range(2):
+        out[far[k]] = (cross[k], [("codes", i, cross[2 * k + i]) for i in range(2)])
+    out[near[0]] = (cross[2], [("scales", i, d) for i, d in enumerate(cross)])
+    out[near[1]] = (cross[3], [("scales", 1 + i, d) for i, d in enumerate(direct)])
+    return out
+
+
+def relay_engines(h, jobs, T, topo):
+    return share(topo.engines(h, T.cores[jobs[0][2]]), len(jobs))
+
+
+def hop_engines(core_r, T, topo):
+    direct, cross, far, near = plan(core_r, T, topo)
+    onc = topo.engines(core_r, far[0])
+    off = topo.engines(core_r, T.cores[direct[0]])
+    return share(onc, 2), share([e for e in onc if e not in off], 2)
+
+
+def arriving(rank, T, topo):
+    ncnt = ncod = nsca = 0
+    for s, c in enumerate(T.cores):
+        if s == rank:
+            continue
+        direct = plan(c, T, topo)[0]
+        if rank in direct:
+            off = topo.engines(c, T.cores[rank])
+            ncnt += len(share(off, len(direct))[0])
+            ncod += len(off)
+        for h, (cd, jobs) in forwards(c, T, topo).items():
+            if cd == rank:
+                ncnt += len(topo.engines(h, T.cores[rank]))
+            for (kind, slot, d), e in zip(jobs, relay_engines(h, jobs, T, topo)):
+                if d == rank and kind == "codes":
+                    ncod += len(e)
+                elif d == rank:
+                    nsca += len(e)
+    return ncnt, ncod, nsca
 
 
 def rank_program(g, core, T, topo):
@@ -87,7 +106,7 @@ def rank_program(g, core, T, topo):
     COPY = ActivationFunctionType.Copy
     V, A, P, Y, S = g.vector, g.scalar, g.tensor, g.sync, T.sem
     direct, cross, far, near = plan(core, T, topo)
-    order = cross + direct + [rank]
+    order = cross + direct
     w32 = dt.uint32
 
     A.dma_start(T.xt[:], T.x[:]).then_inc(S.xl, 16)
@@ -110,14 +129,11 @@ def rank_program(g, core, T, topo):
 
     off = topo.engines(core, T.cores[direct[0]])
     onc = topo.engines(core, far[0])
-    tr = []
-    for k, d in enumerate(direct):
-        tr.append(xfer(T.cores[d], T.rc[:, 4 * rank:4 * rank + 1], T.bc[:, d:d + 1], off[2 * k:2 * k + 2], S.cnt))
-    rest = [e for e in onc if e not in off[:2 * len(direct)]]
-    for k, (d, h) in enumerate(zip(cross, far + near)):
-        part = rest[2 * k:2 * k + 2] if k < len(cross) - 1 else rest[2 * k:2 * k + 4]
-        tr.append(xfer(h, T.hc[:], T.bc[:, d:d + 1], part, S.hci))
-    g.remote_dma_fused(tr, local_sem=S.sent)
+    work = forwards(core, T, topo)
+    g.remote_dma_fused([xfer(h, T.hc[:], T.bc[:, work[h][0]:work[h][0] + 1], e, S.hci)
+                        for h, e in zip(work, share(onc, len(work)))], local_sem=S.sent)
+    g.remote_dma_fused([xfer(T.cores[d], T.rc[:, 4 * rank:4 * rank + 1], T.bc[:, d:d + 1], e, S.cnt)
+                        for d, e in zip(direct, share(off, len(direct)))], local_sem=S.sent)
 
     nv = [0]
 
@@ -130,50 +146,50 @@ def rank_program(g, core, T, topo):
 
     v(V.memset(T.zt[:], 0.0))
     v(V.memset(T.pse[:, 0:1], 0.0))
-    v(V.memset(T.pl[:, 0:1], 0.0))
-    vw()
-    v(V.quantize_mx(T.xq[:, NX:NX + 128], T.xs[:, NX:NX + 128], T.zt[:]))
-    v(V.quantize_mx(T.lq[:, ZC:ZC + 128], T.ls[:, ZC:ZC + 128], T.zt[:]))
     V.wait_ge(S.gi, 2)
     v(V.tensor_scalar(T.pmi[:], T.pidx[:], 15, None, AluOpType.bitwise_and))
     vw()
+    v(V.quantize_mx(T.xq[:, NX:NX + 128], T.xs[:, NX:NX + 128], T.zt[:]))
     v(V.tensor_copy(T.pmf[:], T.pmi[:]))
     vw()
     v(V.tensor_scalar(T.ii[:], T.jj[:], T.pmf[:], None, ADD))
     V.wait_ge(S.bcd, 1)
     v(V.tensor_copy(T.cf[:], T.bc[:]))
-    v(V.tensor_copy(T.rc[:, 4 * rank:4 * rank + 1], T.bc[:, rank:rank + 1]))
     vw()
     v(V.tensor_tensor_scan(T.pse[:, 1:9], T.cf[:], T.cf[:], 0.0, ADD, MAX))
     vw()
     for k, d in enumerate(order):
-        v(V.tensor_scalar(T.lsend[:, 4 * k:4 * k + 4], T.ii[:, 0:4], T.pse[:, d:d + 1], None, ADD))
+        V.tensor_scalar(T.lsend[:, 4 * k:4 * k + 4], T.ii[:, 0:4], T.pse[:, d:d + 1], None, ADD).then_inc(S.ld, 1)
     V.wait_ge(S.xl, 16)
-    vw()
     V.quantize_mx(T.xq[:, 0:NX], T.xs[:, 0:NX], T.xt[:]).then_inc(S.qx, 1)
+    V.wait_ge(S.ld, len(order))
     V.wait_ge(S.qx, 1)
 
     nc = CAP * len(cross)
     nd = CAP * len(direct)
     win = NX + 128
     cuts = [(0, nc, 0, nc // 16), (nc, nc + nd, nc // 16, (nc + nd) // 16)]
-    lo = (nc + nd) // 16
     for (a, b, e, f), sem in zip(cuts, (S.pcx, S.pdx)):
         V.tensor_copy(T.sq[:, a:b].bitcast(w32), T.xq[:, 0:win].bitcast(w32).indirect(T.lsend[:, e:f])).then_inc(sem, 1)
+    V.tensor_scalar(T.lown[:], T.ii[:, 0:4], T.pse[:, rank:rank + 1], None, ADD).then_inc(S.lo, 1)
+    v(V.tensor_copy(T.rc[:, 4 * rank:4 * rank + 1], T.bc[:, rank:rank + 1]))
+    V.wait_ge(S.lo, 1)
     V.tensor_copy(T.lq[:, CAP * rank:CAP * rank + CAP].bitcast(w32),
-                  T.xq[:, 0:win].bitcast(w32).indirect(T.lsend[:, lo:lo + 4])).then_inc(S.own, 1)
+                  T.xq[:, 0:win].bitcast(w32).indirect(T.lown[:, 0:4])).then_inc(S.own, 1)
+    A.wait_ge(S.ld, len(order))
     A.wait_ge(S.qx, 1)
     for (a, b, e, f), sem in zip(cuts, (S.psx, S.psd)):
         A.activation(T.ss[:, a:b], T.xs[:, 0:win].indirect(T.lsend[:, e:f]), COPY).then_inc(sem, 1)
-    A.activation(T.ls[:, CAP * rank:CAP * rank + CAP], T.xs[:, 0:win].indirect(T.lsend[:, lo:lo + 4]), COPY).then_inc(S.owns, 1)
+    A.wait_ge(S.lo, 1)
+    A.activation(T.ls[:, CAP * rank:CAP * rank + CAP], T.xs[:, 0:win].indirect(T.lown[:, 0:4]), COPY).then_inc(S.owns, 1)
 
-    half = len(onc) // 2
+    hopc, hops = hop_engines(core, T, topo)
     g.wait_ge(S.pcx, 1)
     g.remote_dma_fused([xfer(far[k], T.hq[:].bitcast(dt.uint8), T.sq[:, 2 * CAP * k:2 * CAP * (k + 1)].bitcast(dt.uint8),
-                             onc[half * k:half * (k + 1)], S.hqi) for k in range(2)], local_sem=S.sent)
+                             hopc[k], S.hqi) for k in range(2)], local_sem=S.sent)
     g.wait_ge(S.psx, 1)
     g.wait_ge(S.psd, 1)
-    g.remote_dma_fused([xfer(near[k], T.hs[:], T.ss[:, 3 * CAP * k:3 * CAP * k + 4 * CAP], onc[half * k:half * (k + 1)], S.hsi)
+    g.remote_dma_fused([xfer(near[k], T.hs[:], T.ss[:, 3 * CAP * k:3 * CAP * k + 4 * CAP], hops[k], S.hsi)
                         for k in range(2)], local_sem=S.sent)
     g.wait_ge(S.pdx, 1)
     for k, d in enumerate(direct):
@@ -183,29 +199,29 @@ def rank_program(g, core, T, topo):
                      T.sq[:, nc + CAP * k:nc + CAP * k + CAP].bitcast(dt.uint8), S.cod, S.sent, pid, rid, bits(off))
     g.wait_ge(S.sent, sent[0])
 
+    v(V.memset(T.pl[:, 0:1], 0.0))
+    v(V.memset(T.sg[:], 1.0))
+    v(V.quantize_mx(T.lq[:, ZC:ZC + 128], T.ls[:, ZC:ZC + 128], T.zt[:]))
+    v(V.tensor_scalar(T.mk[:, 0:16 * SG:SG], T.jj[:], T.pmf[:], None, ADD))
+    vw()
+    v(V.tensor_scalar(T.sg[:, 0:16 * SG:SG], T.jj[:], 0.0, None, MULT))
     V.wait_ge(S.wl, 16)
     V.quantize_mx(T.wq[:], T.wsc[:], T.wt[:]).then_inc(S.qw, 1)
+
     ncnt, ncod, nsca = arriving(rank, T, topo)
-    V.wait_ge(S.cnt, ncnt)
     vw()
+    V.wait_ge(S.cnt, ncnt)
     v(V.tensor_copy(T.rf[:], T.rc[:, 0:32:4]))
+    v(V.tensor_scalar(T.dd[:], T.rc[:, 0:32:4], -1.0, float(CAP), MULT, ADD))
     vw()
     V.tensor_tensor_scan(T.pl[:, 1:9], T.rf[:], T.rf[:], 0.0, ADD, MAX).then_inc(S.pref, 1)
-    v(V.tensor_scalar(T.dd[:], T.rf[:], -1.0, float(CAP), MULT, ADD))
-    vw()
     V.wait_ge(S.pref, 1)
     for s in range(NR):
-        v(V.tensor_scalar(T.mk[:, 16 * s:16 * s + 16], T.ii[:], T.pl[:, s + 1:s + 2], T.dd[:, s:s + 1], GE, MULT))
+        v(V.tensor_scalar(T.mk[:, 1 + s:16 * SG:SG], T.ii[:], T.pl[:, s + 1:s + 2], T.dd[:, s:s + 1], GE, MULT))
     vw()
-    v(V.tensor_tensor(T.t1[:], T.mk[:, 0:64], T.mk[:, 64:128], ADD))
+    v(V.tensor_tensor_scan(T.sc[:], T.sg[:], T.mk[:], 0.0, MULT, ADD))
     vw()
-    v(V.tensor_tensor(T.t2[:], T.t1[:, 0:32], T.t1[:, 32:64], ADD))
-    vw()
-    v(V.tensor_tensor(T.t3[:], T.t2[:, 0:16], T.t2[:, 16:32], ADD))
-    vw()
-    v(V.tensor_tensor(T.t4[:], T.t3[:], T.ii[:], ADD))
-    vw()
-    V.tensor_scalar(T.lrec[:], T.t4[:], float(ZC), None, MIN).then_inc(S.lr, 1)
+    V.tensor_scalar(T.lrec[:], T.sc[:, NR:16 * SG:SG], float(ZC), None, MIN).then_inc(S.lr, 1)
 
     Y.wait_ge(S.pref, 1)
     Y.dma_start(T.ln[:], T.pl[0:1, 0:9]).then_inc(S.lnd, 16)
@@ -250,40 +266,6 @@ def rank_program(g, core, T, topo):
     vw()
 
 
-def forwards(core_r, T, topo):
-    direct, cross, far, near = plan(core_r, T, topo)
-    out = {}
-    for k in range(2):
-        out[far[k]] = (cross[k], [("codes", i, cross[2 * k + i]) for i in range(2)])
-    out[near[0]] = (cross[2], [("scales", i, d) for i, d in enumerate(cross)])
-    out[near[1]] = (cross[3], [("scales", 1 + i, d) for i, d in enumerate(direct)])
-    return out
-
-
-def relay_engines(h, jobs, T, topo):
-    return share(topo.engines(h, T.cores[jobs[0][2]]), len(jobs))
-
-
-def arriving(rank, T, topo):
-    ncnt = ncod = nsca = 0
-    for s, c in enumerate(T.cores):
-        if s == rank:
-            continue
-        direct, cross, far, near = plan(c, T, topo)
-        if rank in direct:
-            ncnt += 2
-            ncod += len(topo.engines(c, T.cores[rank]))
-        for h, (cd, jobs) in forwards(c, T, topo).items():
-            if cd == rank:
-                ncnt += len(topo.engines(h, T.cores[rank]))
-            for (kind, slot, d), e in zip(jobs, relay_engines(h, jobs, T, topo)):
-                if d == rank and kind == "codes":
-                    ncod += len(e)
-                elif d == rank:
-                    nsca += len(e)
-    return ncnt, ncod, nsca
-
-
 def relay_program(g, core, home, T, topo):
     work = forwards(home, T, topo)
     if core not in work:
@@ -291,18 +273,16 @@ def relay_program(g, core, home, T, topo):
     S = T.sem
     src_rank = T.rank_of(home)
     cd, jobs = work[core]
-    direct, cross, far, near = plan(home, T, topo)
     onc = topo.engines(home, core)
-    half = len(onc) // 2
-    idx = (far + near).index(core)
-    g.wait_ge(S.hci, 2 if idx < 3 else 4)
+    g.wait_ge(S.hci, len(share(onc, len(work))[0]))
     dst = T.cores[cd]
     rid, pid = topo.addr(dst, core)
     eng = topo.engines(core, dst)
     g.remote_dma(T.rc[:, 4 * src_rank:4 * src_rank + 1], T.hc[:], S.cnt, S.sent, pid, rid, bits(eng))
     total = len(eng)
     codes = jobs[0][0] == "codes"
-    g.wait_ge(S.hqi if codes else S.hsi, half)
+    hopc, hops = hop_engines(home, T, topo)
+    g.wait_ge(S.hqi if codes else S.hsi, len(hopc[0]) if codes else len(hops[0]))
     tr = []
     for (kind, slot, d), e in zip(jobs, relay_engines(core, jobs, T, topo)):
         rid, pid = topo.addr(T.cores[d], core)

from concourse.bass import DstId, RemoteDMATransfer
from concourse.mybir import AluOpType, ActivationFunctionType, dt

CAP = 64
NR = 8
NX = 256
ZC = NR * CAP
SG = NR + 1

F8, U8, F32, I32, BF = "float8_e4m3fn_x4", "uint8", "float32", "int32", "bfloat16"
SCRATCH = {name: ("sbuf", [p, n], d) for name, p, n, d in (
    ("xt", 128, 4 * NX, BF), ("wt", 128, 1024, BF), ("zt", 128, 512, BF),
    ("xq", 128, NX + 128, F8), ("xs", 128, NX + 128, U8),
    ("wq", 128, 256, F8), ("wsc", 128, 256, U8),
    ("sq", 128, 7 * CAP, F8), ("ss", 128, 7 * CAP, U8),
    ("hq", 128, 2 * CAP, F8), ("hs", 128, 4 * CAP, U8), ("hc", 128, 1, I32),
    ("lq", 128, ZC + 128, F8), ("ls", 128, ZC + 128, U8),
    ("aq", 128, NX, F8), ("asc", 128, NX, U8),
    ("cnr", 1, 16, I32), ("bc", 128, 8, I32), ("rc", 128, 32, I32),
    ("pidx", 128, 1, I32), ("pmi", 128, 1, I32), ("pmf", 128, 1, F32), ("jj", 128, 16, F32), ("ii", 128, 16, F32),
    ("cf", 128, 8, F32), ("pse", 128, 9, F32), ("lsend", 128, 28, "uint16"), ("lown", 128, 4, "uint16"),
    ("rf", 128, 8, F32), ("pl", 128, 9, F32), ("dd", 128, 8, F32),
    ("mk", 128, 16 * SG, F32), ("sg", 128, 16 * SG, F32), ("sc", 128, 16 * SG, F32), ("lrec", 128, 16, "uint16"),
    ("ysb", 128, 512, F32))}
SCRATCH["ps"] = ("psum", [128, 2048], F32)
SEMAPHORES = ["v", "cnl", "xl", "wl", "gi", "bcd", "qx", "qw", "pcx", "pdx", "psx", "psd", "own", "owns", "pref", "ld", "lo",
              "fa", "fb", "ga", "gb", "m0a", "m1a", "m0b", "m1b", "s0", "s1", "v0", "v1", "lnd", "yd", "zd",
              "sent", "cnt", "cod", "sca", "hci", "hqi", "hsi", "lr"]


def bits(engines):
    return sum(1 << e for e in engines)


def share(engines, n):
    k = 1
    while 2 * k * n <= len(engines):
        k *= 2
    return [engines[i * k:(i + 1) * k] for i in range(n)]


def plan(core_r, T, topo):
    cores = T.cores
    r = T.rank_of(core_r)
    turn = [(r + k) % NR for k in range(1, NR)]
    direct = [d for d in turn if topo.may_write(core_r, cores[d])]
    cross = [d for d in range(NR) if d != r and d not in direct]
    mine = sorted(direct + [r]).index(r)
    cross = cross[mine:] + cross[:mine]
    relays = [h for h in topo.cores_of(core_r) if h != core_r and all(topo.may_write(h, cores[d]) for d in cross)]
    far = [h for h in relays if topo.die(h) != topo.die(core_r)]
    near = [h for h in relays if topo.die(h) == topo.die(core_r)]
    return direct, cross, far, near


def forwards(core_r, T, topo):
    direct, cross, far, near = plan(core_r, T, topo)
    out = {}
    for k in range(2):
        out[far[k]] = (cross[k], [("codes", i, cross[2 * k + i]) for i in range(2)])
    out[near[0]] = (cross[2], [("scales", i, d) for i, d in enumerate(cross)])
    out[near[1]] = (cross[3], [("scales", 1 + i, d) for i, d in enumerate(direct)])
    return out


def relay_engines(h, jobs, T, topo):
    return share(topo.engines(h, T.cores[jobs[0][2]]), len(jobs))


def hop_engines(core_r, T, topo):
    direct, cross, far, near = plan(core_r, T, topo)
    onc = topo.engines(core_r, far[0])
    off = topo.engines(core_r, T.cores[direct[0]])
    return share(onc, 2), share([e for e in onc if e not in off], 2)


def arriving(rank, T, topo):
    ncnt = ncod = nsca = 0
    for s, c in enumerate(T.cores):
        if s == rank:
            continue
        direct = plan(c, T, topo)[0]
        if rank in direct:
            off = topo.engines(c, T.cores[rank])
            ncnt += len(share(off, len(direct))[0])
            ncod += len(off)
        for h, (cd, jobs) in forwards(c, T, topo).items():
            if cd == rank:
                ncnt += len(topo.engines(h, T.cores[rank]))
            for (kind, slot, d), e in zip(jobs, relay_engines(h, jobs, T, topo)):
                if d == rank and kind == "codes":
                    ncod += len(e)
                elif d == rank:
                    nsca += len(e)
    return ncnt, ncod, nsca


def rank_program(g, core, T, topo):
    rank = T.rank_of(core)
    if rank is None:
        for c in T.cores:
            if core in topo.cores_of(c):
                relay_program(g, core, c, T, topo)
        return
    ADD, GE, MULT, MIN, MAX = AluOpType.add, AluOpType.is_ge, AluOpType.mult, AluOpType.min, AluOpType.max
    COPY = ActivationFunctionType.Copy
    V, A, P, Y, S = g.vector, g.scalar, g.tensor, g.sync, T.sem
    direct, cross, far, near = plan(core, T, topo)
    order = cross + direct
    w32 = dt.uint32

    A.dma_start(T.xt[:], T.x[:]).then_inc(S.xl, 16)
    Y.dma_start(T.cnr[0:1, 0:16], T.cn[:]).then_inc(S.cnl, 16)
    Y.wait_ge(S.cnl, 16)
    Y.dma_start(T.wt[:], T.w[:]).then_inc(S.wl, 16)

    g.iota(T.pidx[:], [[1, 1]], 0, 1).then_inc(S.gi, 1)
    g.iota(T.jj[:], [[16, 16]], 0, 0, allow_small_or_imprecise_dtypes=True).then_inc(S.gi, 1)
    g.wait_ge(S.cnl, 16)
    g.partition_broadcast(T.bc[:], T.cnr[0:1, 0:8], 128).then_inc(S.bcd, 1)
    g.wait_ge(S.bcd, 1)
    sent = [0]

    def xfer(dst_core, dst, src, engines, sem):
        rid, pid = topo.addr(dst_core, core)
        sent[0] += len(engines)
        return RemoteDMATransfer(dst_ids=[DstId(rid=rid, pnc=pid)], dma_engine_mask=bits(engines), remote_sem=sem,
                                 srcs=[src], dsts=[dst])

    off = topo.engines(core, T.cores[direct[0]])
    onc = topo.engines(core, far[0])
    work = forwards(core, T, topo)
    g.remote_dma_fused([xfer(h, T.hc[:], T.bc[:, work[h][0]:work[h][0] + 1], e, S.hci)
                        for h, e in zip(work, share(onc, len(work)))], local_sem=S.sent)
    g.remote_dma_fused([xfer(T.cores[d], T.rc[:, 4 * rank:4 * rank + 1], T.bc[:, d:d + 1], e, S.cnt)
                        for d, e in zip(direct, share(off, len(direct)))], local_sem=S.sent)

    nv = [0]

    def v(inst):
        inst.then_inc(S.v, 1)
        nv[0] += 1

    def vw():
        V.wait_ge(S.v, nv[0])

    v(V.memset(T.zt[:], 0.0))
    v(V.memset(T.pse[:, 0:1], 0.0))
    V.wait_ge(S.gi, 2)
    v(V.tensor_scalar(T.pmi[:], T.pidx[:], 15, None, AluOpType.bitwise_and))
    vw()
    v(V.quantize_mx(T.xq[:, NX:NX + 128], T.xs[:, NX:NX + 128], T.zt[:]))
    v(V.tensor_copy(T.pmf[:], T.pmi[:]))
    vw()
    v(V.tensor_scalar(T.ii[:], T.jj[:], T.pmf[:], None, ADD))
    V.wait_ge(S.bcd, 1)
    v(V.tensor_copy(T.cf[:], T.bc[:]))
    vw()
    v(V.tensor_tensor_scan(T.pse[:, 1:9], T.cf[:], T.cf[:], 0.0, ADD, MAX))
    vw()
    for k, d in enumerate(order):
        V.tensor_scalar(T.lsend[:, 4 * k:4 * k + 4], T.ii[:, 0:4], T.pse[:, d:d + 1], None, ADD).then_inc(S.ld, 1)
    V.wait_ge(S.xl, 16)
    V.quantize_mx(T.xq[:, 0:NX], T.xs[:, 0:NX], T.xt[:]).then_inc(S.qx, 1)
    V.wait_ge(S.ld, len(order))
    V.wait_ge(S.qx, 1)

    nc = CAP * len(cross)
    nd = CAP * len(direct)
    win = NX + 128
    cuts = [(0, nc, 0, nc // 16), (nc, nc + nd, nc // 16, (nc + nd) // 16)]
    for (a, b, e, f), sem in zip(cuts, (S.pcx, S.pdx)):
        V.tensor_copy(T.sq[:, a:b].bitcast(w32), T.xq[:, 0:win].bitcast(w32).indirect(T.lsend[:, e:f])).then_inc(sem, 1)
    V.tensor_scalar(T.lown[:], T.ii[:, 0:4], T.pse[:, rank:rank + 1], None, ADD).then_inc(S.lo, 1)
    v(V.tensor_copy(T.rc[:, 4 * rank:4 * rank + 1], T.bc[:, rank:rank + 1]))
    V.wait_ge(S.lo, 1)
    V.tensor_copy(T.lq[:, CAP * rank:CAP * rank + CAP].bitcast(w32),
                  T.xq[:, 0:win].bitcast(w32).indirect(T.lown[:, 0:4])).then_inc(S.own, 1)
    A.wait_ge(S.ld, len(order))
    A.wait_ge(S.qx, 1)
    for (a, b, e, f), sem in zip(cuts, (S.psx, S.psd)):
        A.activation(T.ss[:, a:b], T.xs[:, 0:win].indirect(T.lsend[:, e:f]), COPY).then_inc(sem, 1)
    A.wait_ge(S.lo, 1)
    A.activation(T.ls[:, CAP * rank:CAP * rank + CAP], T.xs[:, 0:win].indirect(T.lown[:, 0:4]), COPY).then_inc(S.owns, 1)

    hopc, hops = hop_engines(core, T, topo)
    g.wait_ge(S.pcx, 1)
    g.remote_dma_fused([xfer(far[k], T.hq[:].bitcast(dt.uint8), T.sq[:, 2 * CAP * k:2 * CAP * (k + 1)].bitcast(dt.uint8),
                             hopc[k], S.hqi) for k in range(2)], local_sem=S.sent)
    g.wait_ge(S.psx, 1)
    g.wait_ge(S.psd, 1)
    g.remote_dma_fused([xfer(near[k], T.hs[:], T.ss[:, 3 * CAP * k:3 * CAP * k + 4 * CAP], hops[k], S.hsi)
                        for k in range(2)], local_sem=S.sent)
    g.wait_ge(S.pdx, 1)
    for k, d in enumerate(direct):
        rid, pid = topo.addr(T.cores[d], core)
        sent[0] += len(off)
        g.remote_dma(T.lq[:, CAP * rank:CAP * rank + CAP].bitcast(dt.uint8),
                     T.sq[:, nc + CAP * k:nc + CAP * k + CAP].bitcast(dt.uint8), S.cod, S.sent, pid, rid, bits(off))
    g.wait_ge(S.sent, sent[0])

    v(V.memset(T.pl[:, 0:1], 0.0))
    v(V.memset(T.sg[:], 1.0))
    v(V.quantize_mx(T.lq[:, ZC:ZC + 128], T.ls[:, ZC:ZC + 128], T.zt[:]))
    v(V.tensor_scalar(T.mk[:, 0:16 * SG:SG], T.jj[:], T.pmf[:], None, ADD))
    vw()
    v(V.tensor_scalar(T.sg[:, 0:16 * SG:SG], T.jj[:], 0.0, None, MULT))
    V.wait_ge(S.wl, 16)
    V.quantize_mx(T.wq[:], T.wsc[:], T.wt[:]).then_inc(S.qw, 1)

    ncnt, ncod, nsca = arriving(rank, T, topo)
    vw()
    V.wait_ge(S.cnt, ncnt)
    v(V.tensor_copy(T.rf[:], T.rc[:, 0:32:4]))
    v(V.tensor_scalar(T.dd[:], T.rc[:, 0:32:4], -1.0, float(CAP), MULT, ADD))
    vw()
    V.tensor_tensor_scan(T.pl[:, 1:9], T.rf[:], T.rf[:], 0.0, ADD, MAX).then_inc(S.pref, 1)
    V.wait_ge(S.pref, 1)
    for s in range(NR):
        v(V.tensor_scalar(T.mk[:, 1 + s:16 * SG:SG], T.ii[:], T.pl[:, s + 1:s + 2], T.dd[:, s:s + 1], GE, MULT))
    vw()
    v(V.tensor_tensor_scan(T.sc[:], T.sg[:], T.mk[:], 0.0, MULT, ADD))
    vw()
    V.tensor_scalar(T.lrec[:], T.sc[:, NR:16 * SG:SG], float(ZC), None, MIN).then_inc(S.lr, 1)

    Y.wait_ge(S.pref, 1)
    Y.dma_start(T.ln[:], T.pl[0:1, 0:9]).then_inc(S.lnd, 16)

    lw = ZC + 128
    V.wait_ge(S.own, 1)
    V.wait_ge(S.lr, 1)
    V.wait_ge(S.cod, ncod)
    for h, sem in enumerate((S.fa, S.fb)):
        V.tensor_copy(T.aq[:, 128 * h:128 * h + 128].bitcast(w32),
                      T.lq[:, 0:lw].bitcast(w32).indirect(T.lrec[:, 8 * h:8 * h + 8])).then_inc(sem, 1)
    A.wait_ge(S.owns, 1)
    A.wait_ge(S.lr, 1)
    A.wait_ge(S.sca, nsca)
    for h, sem in enumerate((S.ga, S.gb)):
        A.activation(T.asc[:, 128 * h:128 * h + 128], T.ls[:, 0:lw].indirect(T.lrec[:, 8 * h:8 * h + 8]), COPY).then_inc(sem, 1)

    P.wait_ge(S.qw, 1)
    for h, (f1, g1, sems) in enumerate(((S.fa, S.ga, (S.m0a, S.m1a)), (S.fb, S.gb, (S.m0b, S.m1b)))):
        P.wait_ge(f1, 1)
        P.wait_ge(g1, 1)
        for o in range(2):
            bank = 512 * (2 * h + o)
            P.matmul_mx(T.ps[:, bank:bank + 128], T.wq[:, 128 * o:128 * o + 128], T.wsc[:, 128 * o:128 * o + 128],
                        T.aq[:, 128 * h:128 * h + 128], T.asc[:, 128 * h:128 * h + 128], True, True).then_inc(sems[o], 1)

    for o, (m, s) in enumerate(((S.m0a, S.s0), (S.m1a, S.s1))):
        A.wait_ge(m, 1)
        A.activation(T.ysb[:, 256 * o:256 * o + 128], T.ps[:, 512 * o:512 * o + 128], COPY).then_inc(s, 1)
    for o, (m, s) in enumerate(((S.m0b, S.v0), (S.m1b, S.v1))):
        V.wait_ge(m, 1)
        V.tensor_copy(T.ysb[:, 256 * o + 128:256 * o + 256], T.ps[:, 1024 + 512 * o:1024 + 512 * o + 128]).then_inc(s, 1)
    Y.wait_ge(S.s0, 1)
    Y.wait_ge(S.v0, 1)
    Y.dma_start(T.y[:, 0:256], T.ysb[:, 0:256]).then_inc(S.yd, 16)
    A.wait_ge(S.s1, 1)
    A.wait_ge(S.v1, 1)
    A.dma_start(T.y[:, 256:512], T.ysb[:, 256:512]).then_inc(S.zd, 16)
    Y.wait_ge(S.yd, 16)
    Y.wait_ge(S.lnd, 16)
    A.wait_ge(S.zd, 16)
    vw()


def relay_program(g, core, home, T, topo):
    work = forwards(home, T, topo)
    if core not in work:
        return
    S = T.sem
    src_rank = T.rank_of(home)
    cd, jobs = work[core]
    onc = topo.engines(home, core)
    g.wait_ge(S.hci, len(share(onc, len(work))[0]))
    dst = T.cores[cd]
    rid, pid = topo.addr(dst, core)
    eng = topo.engines(core, dst)
    g.remote_dma(T.rc[:, 4 * src_rank:4 * src_rank + 1], T.hc[:], S.cnt, S.sent, pid, rid, bits(eng))
    total = len(eng)
    codes = jobs[0][0] == "codes"
    hopc, hops = hop_engines(home, T, topo)
    g.wait_ge(S.hqi if codes else S.hsi, len(hopc[0]) if codes else len(hops[0]))
    tr = []
    for (kind, slot, d), e in zip(jobs, relay_engines(core, jobs, T, topo)):
        rid, pid = topo.addr(T.cores[d], core)
        a, b = CAP * slot, CAP * slot + CAP
        p, q = CAP * src_rank, CAP * src_rank + CAP
        if codes:
            src, dst, sem = T.hq[:, a:b].bitcast(dt.uint8), T.lq[:, p:q].bitcast(dt.uint8), S.cod
        else:
            src, dst, sem = T.hs[:, a:b], T.ls[:, p:q], S.sca
        total += len(e)
        tr.append(RemoteDMATransfer(dst_ids=[DstId(rid=rid, pnc=pid)], dma_engine_mask=bits(e), remote_sem=sem,
                                    srcs=[src], dsts=[dst]))
    g.remote_dma_fused(tr, local_sem=S.sent)
    g.wait_ge(S.sent, total)
